import numpy as np
import ml_dtypes


def mxq(x, axis, fmt="e4m3"):
    dtype, down = {"e4m3": (ml_dtypes.float8_e4m3fn, 7), "e5m2": (ml_dtypes.float8_e5m2, 14)}[fmt]
    v = np.moveaxis(np.asarray(x, np.float32).astype(ml_dtypes.bfloat16).astype(np.float64), axis, -1)
    blocks = v.reshape(v.shape[:-1] + (-1, 32))
    amax = np.abs(blocks).max(-1, keepdims=True)
    byte = np.maximum(np.where(amax > 0, np.frexp(amax)[1] - 1 + 127, 0) - down, 1)
    scale = np.exp2(byte - 127.0)
    codes = (blocks / scale).astype(np.float32).astype(dtype).astype(np.float64)
    return np.moveaxis((codes * scale).reshape(v.shape), -1, axis)


WIDE = False


def mx_kscale(k, group=512):
    if not WIDE:
        return np.ones(k)
    levels = np.array([10, -10, 5, -5, 0])
    if group != 512:
        return np.exp2(np.random.permutation(np.resize(levels, k // group))).repeat(group)
    if k % 512:
        return np.exp2(np.random.permutation(np.resize(levels, k // 32))).repeat(32)
    a = np.empty((k // 512, 16))
    for p in range(k // 512):
        a[p, :8] = np.random.permutation(np.resize(levels, 8))
        for g in range(8):
            far = levels[np.abs(levels - a[p, g]) >= 10]
            a[p, g + 8] = far[np.random.randint(len(far))]
    return np.exp2(a.ravel()).repeat(32)


def f64(x):
    return np.asarray(x).astype(np.float64)


def striped(idx):
    return np.tile(np.asarray(idx).reshape(-1, 16).T, (8, 1)).astype(np.uint16)


def unstriped(offs):
    return offs[:16].T.reshape(-1).astype(np.int64)


H, KV, D, NQ, N = 4, 4, 256, 512, 512
CAP = 2.0


def setup_inputs():
    n = np.random.standard_normal
    s = mx_kscale(D, 0)[:, None]
    u = mx_kscale(N)
    t = np.random.uniform(0.5, 2.0, N) * u
    v = n((KV, N, 128))
    v[:, :, 127] = 1.0
    return {
        "qT": (n((H, D, NQ)) * s * (0.70 / np.sqrt(D))).astype(np.float32),
        "kT": (n((KV, D, N)) / s).astype(np.float32),
        "t": t.reshape(N, 1).astype(np.float32),
        "v": (v / t[:, None]).astype(np.float32),
        "mask": (np.arange(N)[:, None] <= np.sort(np.random.randint(N // 4, N, NQ))[None, :]).astype(np.float32),
    }


def reference(qT, kT, t, v, mask):
    a = mxq(f64(kT), 1, "e4m3").transpose(0, 2, 1) @ mxq(f64(qT), 1, "e4m3")
    a = CAP * np.tanh(a / CAP)
    p = np.square(np.maximum(a, 0.0))
    p = p * f64(mask)
    w = p * f64(t)
    y = mxq(w, 1, "e4m3").transpose(0, 2, 1) @ mxq(f64(v), 1, "e4m3")
    y = y / (y[:, :, 127:128] + 1.0)
    return y

@@ -1,0 +1,250 @@
+from contextlib import ExitStack
+
+import concourse.mybir as mybir
+
+H, D, NQ, N, E = 4, 256, 512, 512, 128
+FLOPS = 2 * H * N * NQ * D + 2 * H * NQ * N * E
+
+F32 = mybir.dt.float32
+BF16 = mybir.dt.bfloat16
+U32 = mybir.dt.uint32
+U8 = mybir.dt.uint8
+X4 = mybir.dt.float8_e4m3fn_x4
+ALU = mybir.AluOpType
+ACT = mybir.ActivationFunctionType
+P = 128
+
+FINE = [7]
+GROUPS = [[0,1],[2,3],[4,5],[6],[7]]
+SCORE_BANKS = 3
+Q_CHUNKS = {0: 128, 1: 128, 2: 256, 4: 256, 6: 256}
+Q_OF_STEP = [0, 1, 2, 2, 4, 4, 6, 6]
+M_CHUNKS = {0: 128, 1: 128, 2: 256}
+ORDER = (
+    "Lt tab Lk0a Lk0b ck0a0:S Lq1 t1 ck0b1:V Lq0 ck0a1:S ck0b0:V qk01 Lq2 cq1:S "
+    "Lm0 Lm1 cq0:S qk00 qq1 qq0 mm1 Lk1b pow mm01 cq2:V mm00 th10 pm0 "
+    "qq2 pm1 th01 Lq4 Lk1a th00 th11 st0 ck1b0:V st1 mm2 cq4:V ck1a0:V Lv0 "
+    "ck1b1:S Lm2 mm3 qq4 th21 sq0:S Lq6 qw0 th20 ck1a1:S qk10 sq1:S th31 th30 "
+    "qk11 cv00 mm4 cv01 pm2 pm3 qv0 mm5 th40 th41 th51 Lv1 cq6:S qw1 "
+    "st3 th50 st2 my0 qq6 st5 cv11 sq3:S st4 sq2:S my1 mm6 sq5:S th60 "
+    "cv10 th61 den0 mm7 qw3 sq4:S qw2 my2 th70 my3 rec0 th71 st6 o0:S "
+    "den1 qw4 rec1 qv1 qw5 o1:S sq6:S st70 st71 my5 W0 my4 W1 den2 "
+    "sq70:V rec2 qw6 o3:S o2:S o5:V W3 sq71:S my6 qw70 qw71 den3 o4:S my70 "
+    "rec3 W5 my71 W2 o6:S W4 den4 rec4 o7:V W6 W7 "
+)
+
+
+def tile_rows_a_relu2_mask_cap_kernel(tc, qT, kT, t, v, mask, out):
+    nc = tc.nc
+    with ExitStack() as ctx:
+        sb = ctx.enter_context(tc.tile_pool(name="sb", bufs=1))
+        ps = ctx.enter_context(tc.psum_pool(name="ps", bufs=1))
+        ctx.enter_context(tc.manual_schedule())
+
+        def tile(name, shape, dtype):
+            return sb.tile(shape, dtype, name=name, align_bytes=64)
+
+        t_sb = tile("t_sb", [P, 4], F32)
+        half = tile("half", [P, 4], F32)
+        warm = tile("warm", [P, 4], F32)
+        sgn01 = tile("sgn01", [P, 4], F32)
+        sgn = tile("sgn", [P, 1, 4, 1], F32)
+        t4 = tile("t4", [P, 4], F32)
+        root = tile("root", [P, 1, 4, 1], F32)
+        k_raw = [[tile("k_raw%d%d" % (g, a), [P, 4, 256], F32) for a in range(2)] for g in range(2)]
+        k_bf = [tile("k_bf%d" % g, [P, 4, P, 4], BF16) for g in range(2)]
+        k_codes = [tile("k_codes%d" % g, [P, N], U32) for g in range(2)]
+        k_scales = [tile("k_scales%d" % g, [P, N], U8) for g in range(2)]
+        q_raw = {s: tile("q_raw%d" % s, [P, 4, w], F32) for s, w in Q_CHUNKS.items()}
+        q_bf = {s: tile("q_bf%d" % s, [P, w, 4], BF16) for s, w in Q_CHUNKS.items()}
+        q_codes = {s: tile("q_codes%d" % s, [P, w], U32) for s, w in Q_CHUNKS.items()}
+        q_scales = {s: tile("q_scales%d" % s, [P, w], U8) for s, w in Q_CHUNKS.items()}
+        m_raw = {c: tile("m_raw%d" % c, [P, 4, w], F32) for c, w in M_CHUNKS.items()}
+        gain = [tile("gain%d" % c, [P, 1, 512], F32) for c in range(4)]
+        v_raw = [tile("v_raw%d" % g, [P, 2, 4, E], F32) for g in range(2)]
+        v_bf = [tile("v_bf%d" % g, [P, 2, E, 4], BF16) for g in range(2)]
+        v_codes = [tile("v_codes%d" % g, [P, 2 * E], U32) for g in range(2)]
+        v_scales = [tile("v_scales%d" % g, [P, 2 * E], U8) for g in range(2)]
+        th = [tile("th%d" % s, [P, 2, 512], F32) for s in range(8)]
+        u = [tile("u%d" % s, [P, 2, 512], F32) for s in range(8)]
+        w_bf = [tile("w_bf%d" % s, [P, 2, 512], BF16) for s in range(8)]
+        w_codes = [tile("w_codes%d" % s, [P, 2 * P], U32) for s in range(8)]
+        w_scales = [tile("w_scales%d" % s, [P, 2 * P], U8) for s in range(8)]
+        den = [tile("den%d" % i, [P, 2 * len(gr), 1], F32) for i, gr in enumerate(GROUPS)]
+        rec = [tile("rec%d" % i, [P, 2 * len(gr), 1], F32) for i, gr in enumerate(GROUPS)]
+        res = [tile("res%d" % s, [P, 2, E], F32) for s in range(8)]
+        score = [[ps.tile([P, 4, P], F32, name="score%d%d" % (h, b)) for b in range(SCORE_BANKS)] for h in range(2)]
+        y = [ps.tile([P, 4, E], F32, name="y%d" % b) for b in range(2)]
+        group_of = {s: i for i, gr in enumerate(GROUPS) for s in gr}
+
+        def flat(ap):
+            return ap.rearrange("p a r b -> p (a r b)")
+
+        def cast(eng, dst, src):
+            if eng == "V":
+                nc.vector.tensor_copy(out=dst, in_=src)
+            else:
+                nc.scalar.copy(out=dst, in_=src)
+
+        def quant(codes, scales, src):
+            nc.vector.quantize_mx(out=codes.bitcast(X4), scales=scales, in_=src)
+
+        def pair(x, g):
+            return x[2 * g : 2 * g + 2].rearrange("h (p j) n -> (h p) j n", j=4)
+
+        def load(n):
+            if n == "t":
+                nc.sync.dma_start(out=t_sb[:], in_=t.rearrange("(p r) o -> p (r o)", r=4))
+            elif n[0] == "q":
+                s = int(n[1])
+                c0 = P * (s % 4)
+                nc.sync.dma_start(out=q_raw[s][:], in_=pair(qT, s // 4)[:, :, c0 : c0 + Q_CHUNKS[s]])
+            elif n[0] == "k":
+                g, a = int(n[1]), "ab".index(n[2])
+                nc.sync.dma_start(out=k_raw[g][a][:], in_=pair(kT, g)[:, :, 256 * a : 256 * a + 256])
+            elif n[0] == "m":
+                c = int(n[1])
+                src = mask.rearrange("(p r) q -> p r q", r=4)
+                nc.sync.dma_start(out=m_raw[c][:], in_=src[:, :, P * c : P * c + M_CHUNKS[c]])
+            else:
+                g = int(n[1])
+                nc.sync.dma_start(out=v_raw[g][:], in_=v[2 * g : 2 * g + 2].rearrange("h (p j) e -> p h j e", j=4))
+
+        def heads(n):
+            return slice(0, 2) if len(n) == 1 else slice(int(n[1]), int(n[1]) + 1)
+
+        def yslot(s, h):
+            i = group_of[s]
+            return y[i % 2], 2 * GROUPS[i].index(s) + h
+
+        for item in ORDER.split():
+            n, eng = (item + ":V").split(":")[:2]
+            kind, arg = n[:2], n[2:]
+            if n[0] == "L":
+                load(n[1:])
+            elif n == "tab":
+                nc.gpsimd.memset(half[:], 0.5)
+                nc.scalar.activation(out=warm[:], in_=half[:], func=ACT.Tanh)
+            elif n == "t1":
+                nc.vector.tensor_scalar(out=sgn01[:], in0=t_sb[:], scalar1=0.0, scalar2=2.0, op0=ALU.is_ge, op1=ALU.mult)
+                nc.vector.tensor_scalar(out=flat(sgn[:]), in0=sgn01[:], scalar1=-1.0, scalar2=None, op0=ALU.add)
+                nc.vector.scalar_tensor_tensor(out=t4[:], in0=t_sb[:], scalar=4.0, in1=flat(sgn[:]), op0=ALU.mult, op1=ALU.mult)
+            elif n == "pow":
+                nc.gpsimd.tensor_tensor(out=flat(root[:]), in0=t4[:], in1=half[:], op=ALU.pow)
+            elif kind == "ck":
+                g, a, x = int(arg[0]), "ab".index(arg[1]), int(arg[2])
+                s0 = 64 * a + 32 * x
+                dst = k_bf[g][:, :, s0 : s0 + 32, :].rearrange("p r s j -> p s j r")
+                src = k_raw[g][a][:, :, P * x : P * x + P].rearrange("p j (s r) -> p s j r", r=4)
+                cast(eng, dst, src)
+            elif kind == "qk":
+                g, x = int(arg[0]), int(arg[1])
+                cols = slice(256 * x, 256 * x + 256)
+                quant(k_codes[g][:, cols], k_scales[g][:, cols], k_bf[g][:, 2 * x : 2 * x + 2].rearrange("p r s j -> p (r s j)"))
+            elif kind == "cq":
+                s = int(arg)
+                cast(eng, q_bf[s][:].rearrange("p (a i) j -> p a j i", i=4), q_raw[s][:].rearrange("p j (a i) -> p a j i", i=4))
+            elif kind == "qq":
+                s = int(arg)
+                quant(q_codes[s][:], q_scales[s][:], q_bf[s][:].rearrange("p n j -> p (n j)"))
+            elif kind == "pm":
+                c = int(arg)
+                src = min(c, 2)
+                c0 = P * (c - src)
+                nc.vector.tensor_tensor(
+                    out=gain[c][:].rearrange("p o (a i r) -> p (o a) r i", i=4, r=4),
+                    in0=m_raw[src][:, :, c0 : c0 + P].rearrange("p r (a i) -> p a r i", i=4),
+                    in1=root[:].to_broadcast([P, 32, 4, 4]),
+                    op=ALU.mult,
+                )
+            elif kind == "cv":
+                g, h = int(arg[0]), int(arg[1])
+                nc.vector.tensor_tensor(
+                    out=v_bf[g][:, h].rearrange("p (a i) j -> p a j i", i=4),
+                    in0=v_raw[g][:, h].rearrange("p j (a i) -> p a j i", i=4),
+                    in1=sgn[:].to_broadcast([P, 32, 4, 4]),
+                    op=ALU.mult,
+                )
+            elif kind == "qv":
+                g = int(arg)
+                quant(v_codes[g][:], v_scales[g][:], v_bf[g][:].rearrange("p h e j -> p (h e j)"))
+            elif kind == "mm":
+                s = int(arg[0])
+                g, qs = s // 4, Q_OF_STEP[s]
+                qc = slice(P * (s - qs), P * (s - qs) + P)
+                for r in range(4) if len(arg) == 1 else range(2 * int(arg[1]), 2 * int(arg[1]) + 2):
+                    kc = slice(P * r, P * r + P)
+                    for h in range(2):
+                        rows = slice(64 * h, 64 * h + 64)
+                        nc.tensor.matmul_mx(
+                            out=score[h][s % SCORE_BANKS][:, r, :],
+                            lhsT=k_codes[g][rows, kc].bitcast(X4),
+                            lhsT_scale=k_scales[g][rows, kc],
+                            rhs=q_codes[qs][rows, qc].bitcast(X4),
+                            rhs_scale=q_scales[qs][rows, qc],
+                            start=True,
+                            stop=True,
+                        )
+            elif kind == "th":
+                s, h = int(arg[0]), int(arg[1])
+                nc.scalar.activation(
+                    out=th[s][:, h, :].rearrange("p (q r) -> p q r", r=4),
+                    in_=score[h][s % SCORE_BANKS][:].rearrange("p r q -> p q r"),
+                    func=ACT.Tanh,
+                    scale=0.5,
+                )
+            elif kind == "st":
+                s, hs = int(arg[0]), heads(arg)
+                nh = hs.stop - hs.start
+                nc.vector.scalar_tensor_tensor(
+                    out=u[s][:, hs, :], in0=th[s][:, hs, :], scalar=0.0,
+                    in1=gain[s % 4][:].to_broadcast([P, nh, 512]), op0=ALU.max, op1=ALU.mult,
+                )
+            elif kind == "sq":
+                s, hs = int(arg[0]), heads(arg)
+                if eng == "V":
+                    nc.vector.tensor_tensor(out=w_bf[s][:, hs, :], in0=u[s][:, hs, :], in1=u[s][:, hs, :], op=ALU.mult)
+                else:
+                    nc.scalar.activation(out=w_bf[s][:, hs, :], in_=u[s][:, hs, :], func=ACT.Square)
+            elif kind == "qw":
+                s, hs = int(arg[0]), heads(arg)
+                cols = slice(P * hs.start, P * hs.stop)
+                quant(w_codes[s][:, cols], w_scales[s][:, cols], w_bf[s][:, hs, :].rearrange("p h n -> p (h n)"))
+            elif kind == "my":
+                s, hs = int(arg[0]), heads(arg)
+                for h in range(hs.start, hs.stop):
+                    bank, slot = yslot(s, h)
+                    cols = slice(P * h, P * h + P)
+                    nc.tensor.matmul_mx(
+                        out=bank[:, slot, :],
+                        lhsT=w_codes[s][:, cols].bitcast(X4),
+                        lhsT_scale=w_scales[s][:, cols],
+                        rhs=v_codes[s // 4][:, cols].bitcast(X4),
+                        rhs_scale=v_scales[s // 4][:, cols],
+                        start=True,
+                        stop=True,
+                    )
+            elif kind == "de":
+                i = int(n[3:])
+                cnt = 2 * len(GROUPS[i])
+                nc.vector.tensor_scalar(out=den[i][:], in0=y[i % 2][:, 0:cnt, E - 1 : E], scalar1=1.0, scalar2=None, op0=ALU.add)
+            elif kind == "re":
+                i = int(n[3:])
+                nc.vector.reciprocal(out=rec[i][:], in_=den[i][:])
+            elif n[0] == "o":
+                s = int(n[1:])
+                i = group_of[s]
+                bank, slot = yslot(s, 0)
+                if eng == "V":
+                    nc.vector.tensor_tensor(
+                        out=res[s][:], in0=bank[:, slot : slot + 2, :],
+                        in1=rec[i][:, slot : slot + 2, :].to_broadcast([P, 2, E]), op=ALU.mult,
+                    )
+                else:
+                    for h in range(2):
+                        nc.scalar.activation(out=res[s][:, h, :], in_=bank[:, slot + h, :], func=ACT.Copy, scale=rec[i][:, slot + h, :])
+            else:
+                s = int(n[1:])
+                g, c = s // 4, s % 4
+                dst = out[2 * g : 2 * g + 2, P * c : P * c + P, :].rearrange("h p e -> p h e")
+                nc.sync.dma_start(out=dst, in_=res[s][:])

@@ -9,28 +9,40 @@ F32 = mybir.dt.float32
 BF16 = mybir.dt.bfloat16
 U32 = mybir.dt.uint32
 U8 = mybir.dt.uint8
-X4 = mybir.dt.float8_e4m3fn_x4
+FP8X4 = mybir.dt.float8_e4m3fn_x4
 ALU = mybir.AluOpType
 ACT = mybir.ActivationFunctionType
-P = 128
 
-FINE = [7]
-GROUPS = [[0,1],[2,3],[4,5],[6],[7]]
-SCORE_BANKS = 3
+P = 128
+PACK = 4
+ROWS = D // PACK
+PAIRS = H // 2
+TILES = NQ // P
+STEPS = PAIRS * TILES
+UNIT = P * PACK
+HALF = N // 2
+SCORE_BANKS = 2
+Y_BANKS = 4
+GROUPS = [[0, 1], [2, 3], [4, 5], [6], [7]]
 Q_CHUNKS = {0: 128, 1: 128, 2: 256, 4: 256, 6: 256}
-Q_OF_STEP = [0, 1, 2, 2, 4, 4, 6, 6]
-M_CHUNKS = {0: 128, 1: 128, 2: 256}
+MASK_CHUNKS = {0: 128, 1: 128, 2: 256}
+SIGN_SCALE = 2.0**120
+
+LOADS = "t k.0.0 k.0.1 q.0 q.1 mask.0 mask.1 q.2 k.1.1 q.4 k.1.0 mask.2 q.6 v.0 v.1"
+
 ORDER = (
-    "Lt tab Lk0a Lk0b ck0a0:S Lq1 t1 ck0b1:V Lq0 ck0a1:S ck0b0:V qk01 Lq2 cq1:S "
-    "Lm0 Lm1 cq0:S qk00 qq1 qq0 mm1 Lk1b pow mm01 cq2:V mm00 th10 pm0 "
-    "qq2 pm1 th01 Lq4 Lk1a th00 th11 st0 ck1b0:V st1 mm2 cq4:V ck1a0:V Lv0 "
-    "ck1b1:S Lm2 mm3 qq4 th21 sq0:S Lq6 qw0 th20 ck1a1:S qk10 sq1:S th31 th30 "
-    "qk11 cv00 mm4 cv01 pm2 pm3 qv0 mm5 th40 th41 th51 Lv1 cq6:S qw1 "
-    "st3 th50 st2 my0 qq6 st5 cv11 sq3:S st4 sq2:S my1 mm6 sq5:S th60 "
-    "cv10 th61 den0 mm7 qw3 sq4:S qw2 my2 th70 my3 rec0 th71 st6 o0:S "
-    "den1 qw4 rec1 qv1 qw5 o1:S sq6:S st70 st71 my5 W0 my4 W1 den2 "
-    "sq70:V rec2 qw6 o3:S o2:S o5:V W3 sq71:S my6 qw70 qw71 den3 o4:S my70 "
-    "rec3 W5 my71 W2 o6:S W4 den4 rec4 o7:V W6 W7 "
+    "t_abs t_clamp t_root t_sign cast_k.0.0.V newton.0 newton.1 cast_k.0.1.V.0 cast_k.0.1.S.1 newton.2 cast_q.0.S.1 "
+    "cast_q.0.V.0 quant_k.0.0 quant_q.0 quant_k.0.1 scores.0.0 scores.0.1 cast_q.1.S quant_q.1 scores.1 "
+    "cap.0.0 make_gain.0 cap.0.1 make_gain.1 cap.1.0 cap.1.1 gate.0.0 square.0.S.0 gate.0.1 cast_q.2.V "
+    "square.0.S.1 gate.1 quant_q.2 cast_q.4.V cast_k.1.1.S quant_w.0.0 quant_w.0.1 scores.2 quant_q.4 "
+    "square.1.S cast_k.1.0.V cap.2.0 cap.2.1 scores.3 cap.3.1 quant_w.1 quant_k.1 make_gain.3 make_gain.2 "
+    "cap.3.0 cast_q.6.S gate.3 gate.2 scores.4 cap.4.0 cap.4.1 cast_v.0.1 scores.5 cap.5.0 quant_q.6 scores.6 "
+    "cap.5.1 cast_v.0.0 square.3.S gate.4 square.2.S quant_v.0 cast_v.1.0 square.4.S gate.5 cast_v.1.1 mix.1 "
+    "quant_w.3 scores.7 mix.0.1 cap.6.0 mix.0.0 quant_w.2 denom.0.V cap.6.1 cap.7.1 mix.3 quant_v.1 recip.0 "
+    "square.5.S gate.6 cap.7.0 quant_w.4 mix.2 divide.0 store.0 mix.4 denom.1.V quant_w.5 square.6.S gate.7.1 "
+    "mix.5 recip.1 divide.1 gate.7.0 divide.2 square.7.S.1 divide.3 denom.2.V quant_w.6 recip.2 store.1 mix.6 "
+    "divide.5 denom.3.S square.7.V.0 quant_w.7.1 mix.7.1 quant_w.7.0 store.2 divide.4 store.3 mix.7.0 recip.3 "
+    "denom.4.V divide.6 store.5 recip.4 divide.7.0 store.4 divide.7.1 store.6 store.7.0 store.7.1 "
 )
 
 
@@ -44,207 +56,249 @@ def tile_rows_a_relu2_mask_cap_kernel(tc, qT, kT, t, v, mask, out):
         def tile(name, shape, dtype):
             return sb.tile(shape, dtype, name=name, align_bytes=64)
 
-        t_sb = tile("t_sb", [P, 4], F32)
-        half = tile("half", [P, 4], F32)
-        warm = tile("warm", [P, 4], F32)
-        sgn01 = tile("sgn01", [P, 4], F32)
-        sgn = tile("sgn", [P, 1, 4, 1], F32)
-        t4 = tile("t4", [P, 4], F32)
-        root = tile("root", [P, 1, 4, 1], F32)
-        k_raw = [[tile("k_raw%d%d" % (g, a), [P, 4, 256], F32) for a in range(2)] for g in range(2)]
-        k_bf = [tile("k_bf%d" % g, [P, 4, P, 4], BF16) for g in range(2)]
-        k_codes = [tile("k_codes%d" % g, [P, N], U32) for g in range(2)]
-        k_scales = [tile("k_scales%d" % g, [P, N], U8) for g in range(2)]
-        q_raw = {s: tile("q_raw%d" % s, [P, 4, w], F32) for s, w in Q_CHUNKS.items()}
-        q_bf = {s: tile("q_bf%d" % s, [P, w, 4], BF16) for s, w in Q_CHUNKS.items()}
-        q_codes = {s: tile("q_codes%d" % s, [P, w], U32) for s, w in Q_CHUNKS.items()}
-        q_scales = {s: tile("q_scales%d" % s, [P, w], U8) for s, w in Q_CHUNKS.items()}
-        m_raw = {c: tile("m_raw%d" % c, [P, 4, w], F32) for c, w in M_CHUNKS.items()}
-        gain = [tile("gain%d" % c, [P, 1, 512], F32) for c in range(4)]
-        v_raw = [tile("v_raw%d" % g, [P, 2, 4, E], F32) for g in range(2)]
-        v_bf = [tile("v_bf%d" % g, [P, 2, E, 4], BF16) for g in range(2)]
-        v_codes = [tile("v_codes%d" % g, [P, 2 * E], U32) for g in range(2)]
-        v_scales = [tile("v_scales%d" % g, [P, 2 * E], U8) for g in range(2)]
-        th = [tile("th%d" % s, [P, 2, 512], F32) for s in range(8)]
-        u = [tile("u%d" % s, [P, 2, 512], F32) for s in range(8)]
-        w_bf = [tile("w_bf%d" % s, [P, 2, 512], BF16) for s in range(8)]
-        w_codes = [tile("w_codes%d" % s, [P, 2 * P], U32) for s in range(8)]
-        w_scales = [tile("w_scales%d" % s, [P, 2 * P], U8) for s in range(8)]
-        den = [tile("den%d" % i, [P, 2 * len(gr), 1], F32) for i, gr in enumerate(GROUPS)]
-        rec = [tile("rec%d" % i, [P, 2 * len(gr), 1], F32) for i, gr in enumerate(GROUPS)]
-        res = [tile("res%d" % s, [P, 2, E], F32) for s in range(8)]
-        score = [[ps.tile([P, 4, P], F32, name="score%d%d" % (h, b)) for b in range(SCORE_BANKS)] for h in range(2)]
-        y = [ps.tile([P, 4, E], F32, name="y%d" % b) for b in range(2)]
-        group_of = {s: i for i, gr in enumerate(GROUPS) for s in gr}
+        t_raw = tile("t_raw", [P, PACK], F32)
+        t_mag = tile("t_mag", [P, PACK], F32)
+        t_clamped = tile("t_clamped", [P, PACK], F32)
+        root_guess = tile("root_guess", [P, PACK], F32)
+        inv_guess = tile("inv_guess", [P, PACK], F32)
+        quotient = tile("quotient", [P, PACK], F32)
+        sign = tile("sign", [P, 1, PACK, 1], F32)
+        root = tile("root", [P, 1, PACK, 1], F32)
 
-        def flat(ap):
-            return ap.rearrange("p a r b -> p (a r b)")
+        k_raw = [[tile("k_raw%d%d" % (g, a), [P, PACK, HALF], F32) for a in range(2)] for g in range(PAIRS)]
+        k_bf = [tile("k_bf%d" % g, [P, PACK, P, PACK], BF16) for g in range(PAIRS)]
+        k_codes = [tile("k_codes%d" % g, [P, N], U32) for g in range(PAIRS)]
+        k_scales = [tile("k_scales%d" % g, [P, N], U8) for g in range(PAIRS)]
+        q_raw = {s: tile("q_raw%d" % s, [P, PACK, width], F32) for s, width in Q_CHUNKS.items()}
+        q_bf = {s: tile("q_bf%d" % s, [P, width, PACK], BF16) for s, width in Q_CHUNKS.items()}
+        q_codes = {s: tile("q_codes%d" % s, [P, width], U32) for s, width in Q_CHUNKS.items()}
+        q_scales = {s: tile("q_scales%d" % s, [P, width], U8) for s, width in Q_CHUNKS.items()}
+        mask_raw = {c: tile("mask_raw%d" % c, [P, PACK, width], F32) for c, width in MASK_CHUNKS.items()}
+        gain = [tile("gain%d" % c, [P, 1, UNIT], F32) for c in range(TILES)]
+        v_raw = [tile("v_raw%d" % g, [P, 2, PACK, E], F32) for g in range(PAIRS)]
+        v_bf = [tile("v_bf%d" % g, [P, 2, E, PACK], BF16) for g in range(PAIRS)]
+        v_codes = [tile("v_codes%d" % g, [P, 2 * E], U32) for g in range(PAIRS)]
+        v_scales = [tile("v_scales%d" % g, [P, 2 * E], U8) for g in range(PAIRS)]
+        capped = [tile("capped%d" % s, [P, 2, UNIT], F32) for s in range(STEPS)]
+        gated = [tile("gated%d" % s, [P, 2, UNIT], F32) for s in range(STEPS)]
+        w_bf = [tile("w_bf%d" % s, [P, 2, UNIT], BF16) for s in range(STEPS)]
+        w_codes = [tile("w_codes%d" % s, [P, 2 * P], U32) for s in range(STEPS)]
+        w_scales = [tile("w_scales%d" % s, [P, 2 * P], U8) for s in range(STEPS)]
+        den = [tile("den%d" % i, [P, 2 * len(group), 1], F32) for i, group in enumerate(GROUPS)]
+        inv_den = [tile("inv_den%d" % i, [P, 2 * len(group), 1], F32) for i, group in enumerate(GROUPS)]
+        result = [tile("result%d" % s, [P, 2, E], F32) for s in range(STEPS)]
 
-        def cast(eng, dst, src):
-            if eng == "V":
+        score = [[ps.tile([P, PACK, P], F32, name="score%d%d" % (h, b)) for b in range(SCORE_BANKS)] for h in range(2)]
+        y = [ps.tile([P, 4, E], F32, name="y%d" % b) for b in range(Y_BANKS)]
+        group_of = {s: i for i, group in enumerate(GROUPS) for s in group}
+
+        def chunk_of(chunks, index):
+            return max(first for first in chunks if first <= index)
+
+        def part(count, half):
+            if half is None:
+                return slice(0, count)
+            return slice(half * count // 2, (half + 1) * count // 2)
+
+        def flat(column):
+            return column[:].rearrange("p a r b -> p (a r b)")
+
+        def pair_view(x, g):
+            return x[2 * g : 2 * g + 2].rearrange("h (p j) n -> (h p) j n", j=PACK)
+
+        def y_slot(s, h):
+            i = group_of[s]
+            return y[i % Y_BANKS][:, 2 * GROUPS[i].index(s) + h, :]
+
+        def copy(engine, dst, src):
+            if engine == "V":
                 nc.vector.tensor_copy(out=dst, in_=src)
             else:
                 nc.scalar.copy(out=dst, in_=src)
 
-        def quant(codes, scales, src):
-            nc.vector.quantize_mx(out=codes.bitcast(X4), scales=scales, in_=src)
+        def quantize(codes, scales, src):
+            nc.vector.quantize_mx(out=codes.bitcast(FP8X4), scales=scales, in_=src)
 
-        def pair(x, g):
-            return x[2 * g : 2 * g + 2].rearrange("h (p j) n -> (h p) j n", j=4)
+        def matmul(dst, lhs_codes, lhs_scales, rhs_codes, rhs_scales):
+            nc.tensor.matmul_mx(
+                out=dst,
+                lhsT=lhs_codes.bitcast(FP8X4),
+                lhsT_scale=lhs_scales,
+                rhs=rhs_codes.bitcast(FP8X4),
+                rhs_scale=rhs_scales,
+                start=True,
+                stop=True,
+            )
 
-        def load(n):
-            if n == "t":
-                nc.sync.dma_start(out=t_sb[:], in_=t.rearrange("(p r) o -> p (r o)", r=4))
-            elif n[0] == "q":
-                s = int(n[1])
-                c0 = P * (s % 4)
-                nc.sync.dma_start(out=q_raw[s][:], in_=pair(qT, s // 4)[:, :, c0 : c0 + Q_CHUNKS[s]])
-            elif n[0] == "k":
-                g, a = int(n[1]), "ab".index(n[2])
-                nc.sync.dma_start(out=k_raw[g][a][:], in_=pair(kT, g)[:, :, 256 * a : 256 * a + 256])
-            elif n[0] == "m":
-                c = int(n[1])
-                src = mask.rearrange("(p r) q -> p r q", r=4)
-                nc.sync.dma_start(out=m_raw[c][:], in_=src[:, :, P * c : P * c + M_CHUNKS[c]])
-            else:
-                g = int(n[1])
-                nc.sync.dma_start(out=v_raw[g][:], in_=v[2 * g : 2 * g + 2].rearrange("h (p j) e -> p h j e", j=4))
+        def load_t():
+            nc.sync.dma_start(out=t_raw[:], in_=t.rearrange("(p r) o -> p (r o)", r=PACK))
 
-        def heads(n):
-            return slice(0, 2) if len(n) == 1 else slice(int(n[1]), int(n[1]) + 1)
+        def load_k(g, a):
+            nc.sync.dma_start(out=k_raw[g][a][:], in_=pair_view(kT, g)[:, :, HALF * a : HALF * (a + 1)])
 
-        def yslot(s, h):
-            i = group_of[s]
-            return y[i % 2], 2 * GROUPS[i].index(s) + h
+        def load_q(s):
+            first = P * (s % TILES)
+            nc.sync.dma_start(out=q_raw[s][:], in_=pair_view(qT, s // TILES)[:, :, first : first + Q_CHUNKS[s]])
 
-        for item in ORDER.split():
-            n, eng = (item + ":V").split(":")[:2]
-            kind, arg = n[:2], n[2:]
-            if n[0] == "L":
-                load(n[1:])
-            elif n == "tab":
-                nc.gpsimd.memset(half[:], 0.5)
-                nc.scalar.activation(out=warm[:], in_=half[:], func=ACT.Tanh)
-            elif n == "t1":
-                nc.vector.tensor_scalar(out=sgn01[:], in0=t_sb[:], scalar1=0.0, scalar2=2.0, op0=ALU.is_ge, op1=ALU.mult)
-                nc.vector.tensor_scalar(out=flat(sgn[:]), in0=sgn01[:], scalar1=-1.0, scalar2=None, op0=ALU.add)
-                nc.vector.scalar_tensor_tensor(out=t4[:], in0=t_sb[:], scalar=4.0, in1=flat(sgn[:]), op0=ALU.mult, op1=ALU.mult)
-            elif n == "pow":
-                nc.gpsimd.tensor_tensor(out=flat(root[:]), in0=t4[:], in1=half[:], op=ALU.pow)
-            elif kind == "ck":
-                g, a, x = int(arg[0]), "ab".index(arg[1]), int(arg[2])
-                s0 = 64 * a + 32 * x
-                dst = k_bf[g][:, :, s0 : s0 + 32, :].rearrange("p r s j -> p s j r")
-                src = k_raw[g][a][:, :, P * x : P * x + P].rearrange("p j (s r) -> p s j r", r=4)
-                cast(eng, dst, src)
-            elif kind == "qk":
-                g, x = int(arg[0]), int(arg[1])
-                cols = slice(256 * x, 256 * x + 256)
-                quant(k_codes[g][:, cols], k_scales[g][:, cols], k_bf[g][:, 2 * x : 2 * x + 2].rearrange("p r s j -> p (r s j)"))
-            elif kind == "cq":
-                s = int(arg)
-                cast(eng, q_bf[s][:].rearrange("p (a i) j -> p a j i", i=4), q_raw[s][:].rearrange("p j (a i) -> p a j i", i=4))
-            elif kind == "qq":
-                s = int(arg)
-                quant(q_codes[s][:], q_scales[s][:], q_bf[s][:].rearrange("p n j -> p (n j)"))
-            elif kind == "pm":
-                c = int(arg)
-                src = min(c, 2)
-                c0 = P * (c - src)
-                nc.vector.tensor_tensor(
-                    out=gain[c][:].rearrange("p o (a i r) -> p (o a) r i", i=4, r=4),
-                    in0=m_raw[src][:, :, c0 : c0 + P].rearrange("p r (a i) -> p a r i", i=4),
-                    in1=root[:].to_broadcast([P, 32, 4, 4]),
-                    op=ALU.mult,
-                )
-            elif kind == "cv":
-                g, h = int(arg[0]), int(arg[1])
-                nc.vector.tensor_tensor(
-                    out=v_bf[g][:, h].rearrange("p (a i) j -> p a j i", i=4),
-                    in0=v_raw[g][:, h].rearrange("p j (a i) -> p a j i", i=4),
-                    in1=sgn[:].to_broadcast([P, 32, 4, 4]),
-                    op=ALU.mult,
-                )
-            elif kind == "qv":
-                g = int(arg)
-                quant(v_codes[g][:], v_scales[g][:], v_bf[g][:].rearrange("p h e j -> p (h e j)"))
-            elif kind == "mm":
-                s = int(arg[0])
-                g, qs = s // 4, Q_OF_STEP[s]
-                qc = slice(P * (s - qs), P * (s - qs) + P)
-                for r in range(4) if len(arg) == 1 else range(2 * int(arg[1]), 2 * int(arg[1]) + 2):
-                    kc = slice(P * r, P * r + P)
-                    for h in range(2):
-                        rows = slice(64 * h, 64 * h + 64)
-                        nc.tensor.matmul_mx(
-                            out=score[h][s % SCORE_BANKS][:, r, :],
-                            lhsT=k_codes[g][rows, kc].bitcast(X4),
-                            lhsT_scale=k_scales[g][rows, kc],
-                            rhs=q_codes[qs][rows, qc].bitcast(X4),
-                            rhs_scale=q_scales[qs][rows, qc],
-                            start=True,
-                            stop=True,
-                        )
-            elif kind == "th":
-                s, h = int(arg[0]), int(arg[1])
-                nc.scalar.activation(
-                    out=th[s][:, h, :].rearrange("p (q r) -> p q r", r=4),
-                    in_=score[h][s % SCORE_BANKS][:].rearrange("p r q -> p q r"),
-                    func=ACT.Tanh,
-                    scale=0.5,
-                )
-            elif kind == "st":
-                s, hs = int(arg[0]), heads(arg)
-                nh = hs.stop - hs.start
+        def load_mask(c):
+            rows = mask.rearrange("(p r) q -> p r q", r=PACK)
+            nc.sync.dma_start(out=mask_raw[c][:], in_=rows[:, :, P * c : P * c + MASK_CHUNKS[c]])
+
+        def load_v(g):
+            nc.sync.dma_start(out=v_raw[g][:], in_=v[2 * g : 2 * g + 2].rearrange("h (p r) e -> p h r e", r=PACK))
+
+        def t_abs():
+            nc.vector.scalar_tensor_tensor(out=t_mag[:], in0=t_raw[:], scalar=-1.0, in1=t_raw[:], op0=ALU.mult, op1=ALU.max)
+
+        def t_clamp():
+            nc.vector.tensor_scalar(out=t_clamped[:], in0=t_raw[:], scalar1=1.0, scalar2=-1.0, op0=ALU.min, op1=ALU.max)
+
+        def t_root():
+            nc.scalar.activation(out=root_guess[:], in_=t_mag[:], func=ACT.Sqrt, scale=4.0)
+
+        def t_sign():
+            nc.scalar.activation(out=flat(sign), in_=t_clamped[:], func=ACT.Tanh, scale=SIGN_SCALE)
+
+        def newton(stage):
+            if stage == 0:
+                nc.vector.reciprocal(out=inv_guess[:], in_=root_guess[:])
+            elif stage == 1:
                 nc.vector.scalar_tensor_tensor(
-                    out=u[s][:, hs, :], in0=th[s][:, hs, :], scalar=0.0,
-                    in1=gain[s % 4][:].to_broadcast([P, nh, 512]), op0=ALU.max, op1=ALU.mult,
+                    out=quotient[:], in0=t_mag[:], scalar=2.0, in1=inv_guess[:], op0=ALU.mult, op1=ALU.mult
                 )
-            elif kind == "sq":
-                s, hs = int(arg[0]), heads(arg)
-                if eng == "V":
-                    nc.vector.tensor_tensor(out=w_bf[s][:, hs, :], in0=u[s][:, hs, :], in1=u[s][:, hs, :], op=ALU.mult)
-                else:
-                    nc.scalar.activation(out=w_bf[s][:, hs, :], in_=u[s][:, hs, :], func=ACT.Square)
-            elif kind == "qw":
-                s, hs = int(arg[0]), heads(arg)
-                cols = slice(P * hs.start, P * hs.stop)
-                quant(w_codes[s][:, cols], w_scales[s][:, cols], w_bf[s][:, hs, :].rearrange("p h n -> p (h n)"))
-            elif kind == "my":
-                s, hs = int(arg[0]), heads(arg)
-                for h in range(hs.start, hs.stop):
-                    bank, slot = yslot(s, h)
-                    cols = slice(P * h, P * h + P)
-                    nc.tensor.matmul_mx(
-                        out=bank[:, slot, :],
-                        lhsT=w_codes[s][:, cols].bitcast(X4),
-                        lhsT_scale=w_scales[s][:, cols],
-                        rhs=v_codes[s // 4][:, cols].bitcast(X4),
-                        rhs_scale=v_scales[s // 4][:, cols],
-                        start=True,
-                        stop=True,
-                    )
-            elif kind == "de":
-                i = int(n[3:])
-                cnt = 2 * len(GROUPS[i])
-                nc.vector.tensor_scalar(out=den[i][:], in0=y[i % 2][:, 0:cnt, E - 1 : E], scalar1=1.0, scalar2=None, op0=ALU.add)
-            elif kind == "re":
-                i = int(n[3:])
-                nc.vector.reciprocal(out=rec[i][:], in_=den[i][:])
-            elif n[0] == "o":
-                s = int(n[1:])
-                i = group_of[s]
-                bank, slot = yslot(s, 0)
-                if eng == "V":
-                    nc.vector.tensor_tensor(
-                        out=res[s][:], in0=bank[:, slot : slot + 2, :],
-                        in1=rec[i][:, slot : slot + 2, :].to_broadcast([P, 2, E]), op=ALU.mult,
-                    )
-                else:
-                    for h in range(2):
-                        nc.scalar.activation(out=res[s][:, h, :], in_=bank[:, slot + h, :], func=ACT.Copy, scale=rec[i][:, slot + h, :])
             else:
-                s = int(n[1:])
-                g, c = s // 4, s % 4
-                dst = out[2 * g : 2 * g + 2, P * c : P * c + P, :].rearrange("h p e -> p h e")
-                nc.sync.dma_start(out=dst, in_=res[s][:])
+                nc.vector.scalar_tensor_tensor(
+                    out=flat(root), in0=root_guess[:], scalar=0.5, in1=quotient[:], op0=ALU.mult, op1=ALU.add
+                )
+
+        def cast_k(g, a, engine, half=None):
+            span = part(P // 2, half)
+            first = (P // 2) * a
+            dst = k_bf[g][:, :, first + span.start : first + span.stop, :].rearrange("p (b e) s j -> p b s j e", e=2)
+            src = k_raw[g][a][:, :, PACK * span.start : PACK * span.stop].rearrange("p j (s b e) -> p b s j e", b=2, e=2)
+            if engine == "V":
+                copy(engine, dst, src)
+            else:
+                for b in range(2):
+                    copy(engine, dst[:, b], src[:, b])
+
+        def quant_k(g, half=None):
+            places = part(PACK, half)
+            cols = slice(P * places.start, P * places.stop)
+            quantize(k_codes[g][:, cols], k_scales[g][:, cols], k_bf[g][:, places].rearrange("p r s j -> p (r s j)"))
+
+        def cast_q(s, engine, half=None):
+            cols = part(Q_CHUNKS[s], half)
+            dst = q_bf[s][:, cols, :].rearrange("p (a e) j -> p a j e", e=2)
+            copy(engine, dst, q_raw[s][:, :, cols].rearrange("p j (a e) -> p a j e", e=2))
+
+        def quant_q(s):
+            quantize(q_codes[s][:], q_scales[s][:], q_bf[s][:].rearrange("p n j -> p (n j)"))
+
+        def make_gain(c):
+            chunk = chunk_of(MASK_CHUNKS, c)
+            first = P * (c - chunk)
+            nc.vector.tensor_tensor(
+                out=gain[c][:].rearrange("p o (a e r) -> p (o a) r e", e=2, r=PACK),
+                in0=mask_raw[chunk][:, :, first : first + P].rearrange("p r (a e) -> p a r e", e=2),
+                in1=root[:].to_broadcast([P, P // 2, PACK, 2]),
+                op=ALU.mult,
+            )
+
+        def cast_v(g, h):
+            nc.vector.tensor_tensor(
+                out=v_bf[g][:, h].rearrange("p (a e) r -> p a r e", e=2),
+                in0=v_raw[g][:, h].rearrange("p r (a e) -> p a r e", e=2),
+                in1=sign[:].to_broadcast([P, E // 2, PACK, 2]),
+                op=ALU.mult,
+            )
+
+        def quant_v(g):
+            quantize(v_codes[g][:], v_scales[g][:], v_bf[g][:].rearrange("p h n r -> p (h n r)"))
+
+        def scores(s, half=None):
+            g, chunk, heads = s // TILES, chunk_of(Q_CHUNKS, s), part(2, half)
+            q_cols = slice(P * (s - chunk), P * (s - chunk + 1))
+            for r in range(PACK):
+                k_cols = slice(P * r, P * (r + 1))
+                for h in range(heads.start, heads.stop):
+                    rows = slice(ROWS * h, ROWS * (h + 1))
+                    matmul(
+                        score[h][s % SCORE_BANKS][:, r, :],
+                        k_codes[g][rows, k_cols],
+                        k_scales[g][rows, k_cols],
+                        q_codes[chunk][rows, q_cols],
+                        q_scales[chunk][rows, q_cols],
+                    )
+
+        def cap(s, h):
+            nc.scalar.activation(
+                out=capped[s][:, h, :].rearrange("p (q r) -> p q r", r=PACK),
+                in_=score[h][s % SCORE_BANKS][:].rearrange("p r q -> p q r"),
+                func=ACT.Tanh,
+                scale=0.5,
+            )
+
+        def gate(s, half=None):
+            heads = part(2, half)
+            nc.vector.scalar_tensor_tensor(
+                out=gated[s][:, heads, :],
+                in0=capped[s][:, heads, :],
+                scalar=0.0,
+                in1=gain[s % TILES][:].to_broadcast([P, heads.stop - heads.start, UNIT]),
+                op0=ALU.max,
+                op1=ALU.mult,
+            )
+
+        def square(s, engine, half=None):
+            heads = part(2, half)
+            src = gated[s][:, heads, :]
+            if engine == "V":
+                nc.vector.tensor_tensor(out=w_bf[s][:, heads, :], in0=src, in1=src, op=ALU.mult)
+            else:
+                nc.scalar.activation(out=w_bf[s][:, heads, :], in_=src, func=ACT.Square)
+
+        def quant_w(s, half=None):
+            heads = part(2, half)
+            cols = slice(P * heads.start, P * heads.stop)
+            quantize(w_codes[s][:, cols], w_scales[s][:, cols], w_bf[s][:, heads, :].rearrange("p h n -> p (h n)"))
+
+        def mix(s, half=None):
+            g, heads = s // TILES, part(2, half)
+            for h in range(heads.start, heads.stop):
+                cols = slice(P * h, P * (h + 1))
+                matmul(y_slot(s, h), w_codes[s][:, cols], w_scales[s][:, cols], v_codes[g][:, cols], v_scales[g][:, cols])
+
+        def denom(i, engine):
+            last_column = y[i % Y_BANKS][:, 0 : 2 * len(GROUPS[i]), E - 1 : E]
+            if engine == "V":
+                nc.vector.tensor_scalar(out=den[i][:], in0=last_column, scalar1=1.0, scalar2=None, op0=ALU.add)
+            else:
+                nc.scalar.activation(out=den[i][:], in_=last_column, func=ACT.Copy, bias=1.0)
+
+        def recip(i):
+            nc.vector.reciprocal(out=inv_den[i][:], in_=den[i][:])
+
+        def divide(s, half=None):
+            i, heads = group_of[s], part(2, half)
+            for h in range(heads.start, heads.stop):
+                factor = inv_den[i][:, 2 * GROUPS[i].index(s) + h, :]
+                nc.scalar.activation(out=result[s][:, h, :], in_=y_slot(s, h), func=ACT.Copy, scale=factor)
+
+        def store(s, half=None):
+            g, c, heads = s // TILES, s % TILES, part(2, half)
+            dst = out[2 * g + heads.start : 2 * g + heads.stop, P * c : P * (c + 1), :].rearrange("h p n -> p h n")
+            nc.sync.dma_start(out=dst, in_=result[s][:, heads, :])
+
+        loads = {"t": load_t, "k": load_k, "q": load_q, "mask": load_mask, "v": load_v}
+        stages = {
+            "t_abs": t_abs, "t_clamp": t_clamp, "t_root": t_root, "t_sign": t_sign, "newton": newton,
+            "cast_k": cast_k, "quant_k": quant_k, "cast_q": cast_q, "quant_q": quant_q,
+            "make_gain": make_gain, "cast_v": cast_v, "quant_v": quant_v,
+            "scores": scores, "cap": cap, "gate": gate, "square": square, "quant_w": quant_w,
+            "mix": mix, "denom": denom, "recip": recip, "divide": divide, "store": store,
+        }
+        for table, entries in ((loads, LOADS), (stages, ORDER)):
+            for entry in entries.split():
+                name, *args = entry.split(".")
+                table[name](*[arg if arg in ("V", "S") else int(arg) for arg in args])

from contextlib import ExitStack

import concourse.mybir as mybir

H, D, NQ, N, E = 4, 256, 512, 512, 128
FLOPS = 2 * H * N * NQ * D + 2 * H * NQ * N * E

F32 = mybir.dt.float32
BF16 = mybir.dt.bfloat16
U32 = mybir.dt.uint32
U8 = mybir.dt.uint8
FP8X4 = mybir.dt.float8_e4m3fn_x4
ALU = mybir.AluOpType
ACT = mybir.ActivationFunctionType

P = 128
PACK = 4
ROWS = D // PACK
PAIRS = H // 2
TILES = NQ // P
STEPS = PAIRS * TILES
UNIT = P * PACK
HALF = N // 2
SCORE_BANKS = 2
Y_BANKS = 4
GROUPS = [[0, 1], [2, 3], [4, 5], [6], [7]]
Q_CHUNKS = {0: 128, 1: 128, 2: 256, 4: 256, 6: 256}
MASK_CHUNKS = {0: 128, 1: 128, 2: 256}
SIGN_SCALE = 2.0**120

LOADS = "t k.0.0 k.0.1 q.0 q.1 mask.0 mask.1 q.2 k.1.1 q.4 k.1.0 mask.2 q.6 v.0 v.1"

ORDER = (
    "t_abs t_clamp t_root t_sign cast_k.0.0.V newton.0 newton.1 cast_k.0.1.V.0 cast_k.0.1.S.1 newton.2 cast_q.0.S.1 "
    "cast_q.0.V.0 quant_k.0.0 quant_q.0 quant_k.0.1 scores.0.0 scores.0.1 cast_q.1.S quant_q.1 scores.1 "
    "cap.0.0 make_gain.0 cap.0.1 make_gain.1 cap.1.0 cap.1.1 gate.0.0 square.0.S.0 gate.0.1 cast_q.2.V "
    "square.0.S.1 gate.1 quant_q.2 cast_q.4.V cast_k.1.1.S quant_w.0.0 quant_w.0.1 scores.2 quant_q.4 "
    "square.1.S cast_k.1.0.V cap.2.0 cap.2.1 scores.3 cap.3.1 quant_w.1 quant_k.1 make_gain.3 make_gain.2 "
    "cap.3.0 cast_q.6.S gate.3 gate.2 scores.4 cap.4.0 cap.4.1 cast_v.0.1 scores.5 cap.5.0 quant_q.6 scores.6 "
    "cap.5.1 cast_v.0.0 square.3.S gate.4 square.2.S quant_v.0 cast_v.1.0 square.4.S gate.5 cast_v.1.1 mix.1 "
    "quant_w.3 scores.7 mix.0.1 cap.6.0 mix.0.0 quant_w.2 denom.0.V cap.6.1 cap.7.1 mix.3 quant_v.1 recip.0 "
    "square.5.S gate.6 cap.7.0 quant_w.4 mix.2 divide.0 store.0 mix.4 denom.1.V quant_w.5 square.6.S gate.7.1 "
    "mix.5 recip.1 divide.1 gate.7.0 divide.2 square.7.S.1 divide.3 denom.2.V quant_w.6 recip.2 store.1 mix.6 "
    "divide.5 denom.3.S square.7.V.0 quant_w.7.1 mix.7.1 quant_w.7.0 store.2 divide.4 store.3 mix.7.0 recip.3 "
    "denom.4.V divide.6 store.5 recip.4 divide.7.0 store.4 divide.7.1 store.6 store.7.0 store.7.1 "
)


def tile_rows_a_relu2_mask_cap_kernel(tc, qT, kT, t, v, mask, out):
    nc = tc.nc
    with ExitStack() as ctx:
        sb = ctx.enter_context(tc.tile_pool(name="sb", bufs=1))
        ps = ctx.enter_context(tc.psum_pool(name="ps", bufs=1))
        ctx.enter_context(tc.manual_schedule())

        def tile(name, shape, dtype):
            return sb.tile(shape, dtype, name=name, align_bytes=64)

        t_raw = tile("t_raw", [P, PACK], F32)
        t_mag = tile("t_mag", [P, PACK], F32)
        t_clamped = tile("t_clamped", [P, PACK], F32)
        root_guess = tile("root_guess", [P, PACK], F32)
        inv_guess = tile("inv_guess", [P, PACK], F32)
        quotient = tile("quotient", [P, PACK], F32)
        sign = tile("sign", [P, 1, PACK, 1], F32)
        root = tile("root", [P, 1, PACK, 1], F32)

        k_raw = [[tile("k_raw%d%d" % (g, a), [P, PACK, HALF], F32) for a in range(2)] for g in range(PAIRS)]
        k_bf = [tile("k_bf%d" % g, [P, PACK, P, PACK], BF16) for g in range(PAIRS)]
        k_codes = [tile("k_codes%d" % g, [P, N], U32) for g in range(PAIRS)]
        k_scales = [tile("k_scales%d" % g, [P, N], U8) for g in range(PAIRS)]
        q_raw = {s: tile("q_raw%d" % s, [P, PACK, width], F32) for s, width in Q_CHUNKS.items()}
        q_bf = {s: tile("q_bf%d" % s, [P, width, PACK], BF16) for s, width in Q_CHUNKS.items()}
        q_codes = {s: tile("q_codes%d" % s, [P, width], U32) for s, width in Q_CHUNKS.items()}
        q_scales = {s: tile("q_scales%d" % s, [P, width], U8) for s, width in Q_CHUNKS.items()}
        mask_raw = {c: tile("mask_raw%d" % c, [P, PACK, width], F32) for c, width in MASK_CHUNKS.items()}
        gain = [tile("gain%d" % c, [P, 1, UNIT], F32) for c in range(TILES)]
        v_raw = [tile("v_raw%d" % g, [P, 2, PACK, E], F32) for g in range(PAIRS)]
        v_bf = [tile("v_bf%d" % g, [P, 2, E, PACK], BF16) for g in range(PAIRS)]
        v_codes = [tile("v_codes%d" % g, [P, 2 * E], U32) for g in range(PAIRS)]
        v_scales = [tile("v_scales%d" % g, [P, 2 * E], U8) for g in range(PAIRS)]
        capped = [tile("capped%d" % s, [P, 2, UNIT], F32) for s in range(STEPS)]
        gated = [tile("gated%d" % s, [P, 2, UNIT], F32) for s in range(STEPS)]
        w_bf = [tile("w_bf%d" % s, [P, 2, UNIT], BF16) for s in range(STEPS)]
        w_codes = [tile("w_codes%d" % s, [P, 2 * P], U32) for s in range(STEPS)]
        w_scales = [tile("w_scales%d" % s, [P, 2 * P], U8) for s in range(STEPS)]
        den = [tile("den%d" % i, [P, 2 * len(group), 1], F32) for i, group in enumerate(GROUPS)]
        inv_den = [tile("inv_den%d" % i, [P, 2 * len(group), 1], F32) for i, group in enumerate(GROUPS)]
        result = [tile("result%d" % s, [P, 2, E], F32) for s in range(STEPS)]

        score = [[ps.tile([P, PACK, P], F32, name="score%d%d" % (h, b)) for b in range(SCORE_BANKS)] for h in range(2)]
        y = [ps.tile([P, 4, E], F32, name="y%d" % b) for b in range(Y_BANKS)]
        group_of = {s: i for i, group in enumerate(GROUPS) for s in group}

        def chunk_of(chunks, index):
            return max(first for first in chunks if first <= index)

        def part(count, half):
            if half is None:
                return slice(0, count)
            return slice(half * count // 2, (half + 1) * count // 2)

        def flat(column):
            return column[:].rearrange("p a r b -> p (a r b)")

        def pair_view(x, g):
            return x[2 * g : 2 * g + 2].rearrange("h (p j) n -> (h p) j n", j=PACK)

        def y_slot(s, h):
            i = group_of[s]
            return y[i % Y_BANKS][:, 2 * GROUPS[i].index(s) + h, :]

        def copy(engine, dst, src):
            if engine == "V":
                nc.vector.tensor_copy(out=dst, in_=src)
            else:
                nc.scalar.copy(out=dst, in_=src)

        def quantize(codes, scales, src):
            nc.vector.quantize_mx(out=codes.bitcast(FP8X4), scales=scales, in_=src)

        def matmul(dst, lhs_codes, lhs_scales, rhs_codes, rhs_scales):
            nc.tensor.matmul_mx(
                out=dst,
                lhsT=lhs_codes.bitcast(FP8X4),
                lhsT_scale=lhs_scales,
                rhs=rhs_codes.bitcast(FP8X4),
                rhs_scale=rhs_scales,
                start=True,
                stop=True,
            )

        def load_t():
            nc.sync.dma_start(out=t_raw[:], in_=t.rearrange("(p r) o -> p (r o)", r=PACK))

        def load_k(g, a):
            nc.sync.dma_start(out=k_raw[g][a][:], in_=pair_view(kT, g)[:, :, HALF * a : HALF * (a + 1)])

        def load_q(s):
            first = P * (s % TILES)
            nc.sync.dma_start(out=q_raw[s][:], in_=pair_view(qT, s // TILES)[:, :, first : first + Q_CHUNKS[s]])

        def load_mask(c):
            rows = mask.rearrange("(p r) q -> p r q", r=PACK)
            nc.sync.dma_start(out=mask_raw[c][:], in_=rows[:, :, P * c : P * c + MASK_CHUNKS[c]])

        def load_v(g):
            nc.sync.dma_start(out=v_raw[g][:], in_=v[2 * g : 2 * g + 2].rearrange("h (p r) e -> p h r e", r=PACK))

        def t_abs():
            nc.vector.scalar_tensor_tensor(out=t_mag[:], in0=t_raw[:], scalar=-1.0, in1=t_raw[:], op0=ALU.mult, op1=ALU.max)

        def t_clamp():
            nc.vector.tensor_scalar(out=t_clamped[:], in0=t_raw[:], scalar1=1.0, scalar2=-1.0, op0=ALU.min, op1=ALU.max)

        def t_root():
            nc.scalar.activation(out=root_guess[:], in_=t_mag[:], func=ACT.Sqrt, scale=4.0)

        def t_sign():
            nc.scalar.activation(out=flat(sign), in_=t_clamped[:], func=ACT.Tanh, scale=SIGN_SCALE)

        def newton(stage):
            if stage == 0:
                nc.vector.reciprocal(out=inv_guess[:], in_=root_guess[:])
            elif stage == 1:
                nc.vector.scalar_tensor_tensor(
                    out=quotient[:], in0=t_mag[:], scalar=2.0, in1=inv_guess[:], op0=ALU.mult, op1=ALU.mult
                )
            else:
                nc.vector.scalar_tensor_tensor(
                    out=flat(root), in0=root_guess[:], scalar=0.5, in1=quotient[:], op0=ALU.mult, op1=ALU.add
                )

        def cast_k(g, a, engine, half=None):
            span = part(P // 2, half)
            first = (P // 2) * a
            dst = k_bf[g][:, :, first + span.start : first + span.stop, :].rearrange("p (b e) s j -> p b s j e", e=2)
            src = k_raw[g][a][:, :, PACK * span.start : PACK * span.stop].rearrange("p j (s b e) -> p b s j e", b=2, e=2)
            if engine == "V":
                copy(engine, dst, src)
            else:
                for b in range(2):
                    copy(engine, dst[:, b], src[:, b])

        def quant_k(g, half=None):
            places = part(PACK, half)
            cols = slice(P * places.start, P * places.stop)
            quantize(k_codes[g][:, cols], k_scales[g][:, cols], k_bf[g][:, places].rearrange("p r s j -> p (r s j)"))

        def cast_q(s, engine, half=None):
            cols = part(Q_CHUNKS[s], half)
            dst = q_bf[s][:, cols, :].rearrange("p (a e) j -> p a j e", e=2)
            copy(engine, dst, q_raw[s][:, :, cols].rearrange("p j (a e) -> p a j e", e=2))

        def quant_q(s):
            quantize(q_codes[s][:], q_scales[s][:], q_bf[s][:].rearrange("p n j -> p (n j)"))

        def make_gain(c):
            chunk = chunk_of(MASK_CHUNKS, c)
            first = P * (c - chunk)
            nc.vector.tensor_tensor(
                out=gain[c][:].rearrange("p o (a e r) -> p (o a) r e", e=2, r=PACK),
                in0=mask_raw[chunk][:, :, first : first + P].rearrange("p r (a e) -> p a r e", e=2),
                in1=root[:].to_broadcast([P, P // 2, PACK, 2]),
                op=ALU.mult,
            )

        def cast_v(g, h):
            nc.vector.tensor_tensor(
                out=v_bf[g][:, h].rearrange("p (a e) r -> p a r e", e=2),
                in0=v_raw[g][:, h].rearrange("p r (a e) -> p a r e", e=2),
                in1=sign[:].to_broadcast([P, E // 2, PACK, 2]),
                op=ALU.mult,
            )

        def quant_v(g):
            quantize(v_codes[g][:], v_scales[g][:], v_bf[g][:].rearrange("p h n r -> p (h n r)"))

        def scores(s, half=None):
            g, chunk, heads = s // TILES, chunk_of(Q_CHUNKS, s), part(2, half)
            q_cols = slice(P * (s - chunk), P * (s - chunk + 1))
            for r in range(PACK):
                k_cols = slice(P * r, P * (r + 1))
                for h in range(heads.start, heads.stop):
                    rows = slice(ROWS * h, ROWS * (h + 1))
                    matmul(
                        score[h][s % SCORE_BANKS][:, r, :],
                        k_codes[g][rows, k_cols],
                        k_scales[g][rows, k_cols],
                        q_codes[chunk][rows, q_cols],
                        q_scales[chunk][rows, q_cols],
                    )

        def cap(s, h):
            nc.scalar.activation(
                out=capped[s][:, h, :].rearrange("p (q r) -> p q r", r=PACK),
                in_=score[h][s % SCORE_BANKS][:].rearrange("p r q -> p q r"),
                func=ACT.Tanh,
                scale=0.5,
            )

        def gate(s, half=None):
            heads = part(2, half)
            nc.vector.scalar_tensor_tensor(
                out=gated[s][:, heads, :],
                in0=capped[s][:, heads, :],
                scalar=0.0,
                in1=gain[s % TILES][:].to_broadcast([P, heads.stop - heads.start, UNIT]),
                op0=ALU.max,
                op1=ALU.mult,
            )

        def square(s, engine, half=None):
            heads = part(2, half)
            src = gated[s][:, heads, :]
            if engine == "V":
                nc.vector.tensor_tensor(out=w_bf[s][:, heads, :], in0=src, in1=src, op=ALU.mult)
            else:
                nc.scalar.activation(out=w_bf[s][:, heads, :], in_=src, func=ACT.Square)

        def quant_w(s, half=None):
            heads = part(2, half)
            cols = slice(P * heads.start, P * heads.stop)
            quantize(w_codes[s][:, cols], w_scales[s][:, cols], w_bf[s][:, heads, :].rearrange("p h n -> p (h n)"))

        def mix(s, half=None):
            g, heads = s // TILES, part(2, half)
            for h in range(heads.start, heads.stop):
                cols = slice(P * h, P * (h + 1))
                matmul(y_slot(s, h), w_codes[s][:, cols], w_scales[s][:, cols], v_codes[g][:, cols], v_scales[g][:, cols])

        def denom(i, engine):
            last_column = y[i % Y_BANKS][:, 0 : 2 * len(GROUPS[i]), E - 1 : E]
            if engine == "V":
                nc.vector.tensor_scalar(out=den[i][:], in0=last_column, scalar1=1.0, scalar2=None, op0=ALU.add)
            else:
                nc.scalar.activation(out=den[i][:], in_=last_column, func=ACT.Copy, bias=1.0)

        def recip(i):
            nc.vector.reciprocal(out=inv_den[i][:], in_=den[i][:])

        def divide(s, half=None):
            i, heads = group_of[s], part(2, half)
            for h in range(heads.start, heads.stop):
                factor = inv_den[i][:, 2 * GROUPS[i].index(s) + h, :]
                nc.scalar.activation(out=result[s][:, h, :], in_=y_slot(s, h), func=ACT.Copy, scale=factor)

        def store(s, half=None):
            g, c, heads = s // TILES, s % TILES, part(2, half)
            dst = out[2 * g + heads.start : 2 * g + heads.stop, P * c : P * (c + 1), :].rearrange("h p n -> p h n")
            nc.sync.dma_start(out=dst, in_=result[s][:, heads, :])

        loads = {"t": load_t, "k": load_k, "q": load_q, "mask": load_mask, "v": load_v}
        stages = {
            "t_abs": t_abs, "t_clamp": t_clamp, "t_root": t_root, "t_sign": t_sign, "newton": newton,
            "cast_k": cast_k, "quant_k": quant_k, "cast_q": cast_q, "quant_q": quant_q,
            "make_gain": make_gain, "cast_v": cast_v, "quant_v": quant_v,
            "scores": scores, "cap": cap, "gate": gate, "square": square, "quant_w": quant_w,
            "mix": mix, "denom": denom, "recip": recip, "divide": divide, "store": store,
        }
        for table, entries in ((loads, LOADS), (stages, ORDER)):
            for entry in entries.split():
                name, *args = entry.split(".")
                table[name](*[arg if arg in ("V", "S") else int(arg) for arg in args])
